import numpy as np
import ml_dtypes


def mxq(x, axis, fmt="e4m3"):
    dtype, down = {"e4m3": (ml_dtypes.float8_e4m3fn, 7), "e5m2": (ml_dtypes.float8_e5m2, 14)}[fmt]
    v = np.moveaxis(np.asarray(x, np.float32).astype(ml_dtypes.bfloat16).astype(np.float64), axis, -1)
    blocks = v.reshape(v.shape[:-1] + (-1, 32))
    amax = np.abs(blocks).max(-1, keepdims=True)
    byte = np.maximum(np.where(amax > 0, np.frexp(amax)[1] - 1 + 127, 0) - down, 1)
    scale = np.exp2(byte - 127.0)
    codes = (blocks / scale).astype(np.float32).astype(dtype).astype(np.float64)
    return np.moveaxis((codes * scale).reshape(v.shape), -1, axis)


WIDE = False


def mx_kscale(k):
    if not WIDE:
        return np.ones(k)
    levels = np.array([10, -10, 5, -5, 0])
    if k % 512:
        return np.exp2(np.random.permutation(np.resize(levels, k // 32))).repeat(32)
    a = np.empty((k // 512, 16))
    for p in range(k // 512):
        a[p, :8] = np.random.permutation(np.resize(levels, 8))
        for g in range(8):
            far = levels[np.abs(levels - a[p, g]) >= 10]
            a[p, g + 8] = far[np.random.randint(len(far))]
    return np.exp2(a.ravel()).repeat(32)


def f64(x):
    return np.asarray(x).astype(np.float64)


def striped(idx):
    return np.tile(idx.reshape(-1, 16).T, (8, 1)).astype(np.uint16)


def unstriped(offs):
    return offs[:16].T.reshape(-1).astype(np.int64)


E2M1 = np.array([0.0, 0.5, 1.0, 1.5, 2.0, 3.0, 4.0, 6.0, -0.0, -0.5, -1.0, -1.5, -2.0, -3.0, -4.0, -6.0])


def pack_weight(w, fmt):
    k, n = w.shape
    w = f64(np.asarray(w, np.float32).astype(ml_dtypes.bfloat16)).reshape(k // 32, 32, n)
    amax = np.abs(w).max(1)
    if fmt == "e4m3":
        byte = np.frexp(amax)[1] - 1 + 127 - 7
    else:
        mant, ex = np.frexp(amax / 6.0)
        byte = np.where(mant > 0.5, ex, ex - 1) + 127
    byte = np.clip(np.where(amax > 0, byte, 1), 1, 254)
    scaled = (w * np.exp2(127.0 - byte)[:, None, :]).reshape(k, n).astype(np.float32)
    by_word = np.ascontiguousarray(scaled.reshape(k // 512, 128, 4, n).transpose(0, 1, 3, 2))
    if fmt == "e4m3":
        words = by_word.astype(ml_dtypes.float8_e4m3fn).view(np.uint8)
    else:
        c = by_word.astype(ml_dtypes.float4_e2m1fn).view(np.uint8) & 0xF
        words = (c[..., 0::2] | (c[..., 1::2] << 4)).reshape(k // 512, 128, 2 * n)
    return np.ascontiguousarray(words), np.ascontiguousarray(byte.astype(np.uint8).reshape(k // 512, 16, n))


def unpack_weight(words, scales, fmt):
    g, _, n = scales.shape
    words = np.ascontiguousarray(words).reshape(g, 128, n, -1)
    if fmt == "e4m3":
        vals = words.view(ml_dtypes.float8_e4m3fn).astype(np.float64)
    else:
        nib = np.empty((g, 128, n, 4), np.uint8)
        nib[..., 0::2] = words & 0xF
        nib[..., 1::2] = words >> 4
        vals = E2M1[nib]
    vals = vals * np.repeat(np.exp2(scales.astype(np.float64) - 127.0), 8, axis=1)[..., None]
    return vals.transpose(0, 1, 3, 2).reshape(g * 512, n)


def gelu(v):
    return 0.5 * v * (1.0 + np.tanh(np.sqrt(2.0 / np.pi) * (v + 0.044715 * v**3)))


def striped8(idx):
    return np.concatenate([v.reshape(-1, 16).T for v in idx]).astype(np.uint16)


def unstriped8(offs):
    return np.stack([offs[16 * g:16 * g + 16].T.reshape(-1) for g in range(8)]).astype(np.int64)


def heads(h, wgt, idx8):
    r = np.arange(h.shape[0])
    return wgt[r // 4 % 128] * h[r[:, None], idx8[r % 512 // 64]]


def put_heads(h, wgs, idx8, t2):
    r = np.arange(h.shape[0])
    page = np.zeros((h.shape[0], t2))
    page[r[:, None], idx8[r % 512 // 64]] = wgs[r // 4 % 128] * h
    return page


K, T, S, H, P, T2, N = 512, 4096, 1024, 1024, 512, 1024, 512


def setup_inputs():
    n = np.random.standard_normal
    s = mx_kscale(K)[:, None]
    u = mx_kscale(H)[:, None]
    d = {}
    d["tab_words"], d["tab_scales"] = pack_weight(n((K, T)) * s, "e4m3")
    d["offs"] = striped(np.random.permutation(T)[:S])
    d["wfoam"] = (n((K, H)) / K**0.5 / s * u.T).astype(np.float32)
    d["wplume"] = None
    d.pop("wplume")
    d["wplume_words"], d["wplume_scales"] = pack_weight(n((K, H)) / K**0.5 / s * u.T, "e2m1")
    d["wview"] = (n((K, H)) / K**0.5 / s * u.T).astype(np.float32)
    d["offs2"] = striped8(np.stack([np.random.permutation(S)[:P] for _ in range(8)]))
    d["wgt"] = np.repeat(np.random.uniform(0.5, 2.0, (8, P)), 16, axis=0).astype(np.float32)
    d["shore"] = (0.6 * n(H) * u[:, 0]).astype(np.float32)
    d["whaz_words"], d["whaz_scales"] = pack_weight(1.2 * n((H, N)) / H**0.5 / u, "e4m3")
    d["tide"] = (0.8 * n((N, P))).astype(np.float32)
    d["offs3"] = striped8(np.stack([np.random.permutation(T2)[:P] for _ in range(8)]))
    d["wgo"] = np.repeat(np.random.uniform(0.5, 2.0, (8, P)), 16, axis=0).astype(np.float32)
    return d


def reference(tab_words, tab_scales, offs, wfoam, wplume_words, wplume_scales, wview, offs2, wgt,
              shore, whaz_words, whaz_scales, tide, offs3, wgo):
    v = unpack_weight(tab_words, tab_scales, "e4m3")[:, unstriped(offs)]
    foam = mxq(f64(wfoam), 0, "e4m3").T @ v
    plume = unpack_weight(wplume_words, wplume_scales, "e2m1").T @ v
    view = mxq(f64(wview), 0, "e4m3").T @ v
    h = np.minimum(np.maximum(foam, plume), view)
    x = heads(h, f64(wgt), unstriped8(offs2)) + f64(shore)[:, None]
    q = unpack_weight(whaz_words, whaz_scales, "e4m3").T @ mxq(x, 0, "e4m3")
    y = q * f64(tide) + np.tanh(q)
    return put_heads(y, f64(wgo), unstriped8(offs3), T2)

@@ -1,0 +1,267 @@
+from contextlib import ExitStack
+
+import concourse.mybir as mybir
+from concourse.masks import make_identity
+
+K, T, S, H, M, T2, N = 512, 4096, 1024, 1024, 512, 1024, 512
+FLOPS = 2 * (3 * K * H * S + H * N * M)
+
+F32 = mybir.dt.float32
+BF16 = mybir.dt.bfloat16
+I32 = mybir.dt.int32
+U32 = mybir.dt.uint32
+U16 = mybir.dt.uint16
+U8 = mybir.dt.uint8
+FP8X4 = mybir.dt.float8_e4m3fn_x4
+FP4X4 = mybir.dt.float4_e2m1fn_x4
+ALU = mybir.AluOpType
+ACT = mybir.ActivationFunctionType
+
+P = 128
+PACK = 4
+KP = P * PACK
+BANK = 512
+HALF = M // 2
+OFFS_COLS = HALF // 16
+
+
+def tile_list_rip_current_watch_kernel(tc, tab_words, tab_scales, offs, wfoam, wplume_words, wplume_scales,
+                                                 wview, offs2, wgt, shore, whaz_words, whaz_scales, tide, offs3, wgo,
+                                                 out):
+    nc = tc.nc
+    blocks = H // KP
+    with ExitStack() as ctx:
+        keep = ctx.enter_context(tc.tile_pool(name="keep", bufs=1))
+        ring = ctx.enter_context(tc.tile_pool(name="ring", bufs=2))
+        psum = ctx.enter_context(tc.psum_pool(name="psum", bufs=1))
+
+        def held(shape, dtype, name):
+            return keep.tile(shape, dtype, name=name, align_bytes=64)
+
+        def load_scale_rows(plane, rows):
+            for r in range(4):
+                nc.sync.dma_start(plane[r:P:32, :], rows[r])
+
+        tab_plane = held([P, T // 4], I32, "tab_plane")
+        plume_plane_raw = held([P, H // 4], I32, "plume_plane_raw")
+        haz_plane = held([P, blocks * N // 4], I32, "haz_plane")
+        pages = [held([P, T2], F32, f"page{i}") for i in range(PACK)]
+        for plane in (tab_plane, plume_plane_raw, haz_plane):
+            nc.vector.memset(plane[:], 0)
+        for page in pages:
+            nc.vector.memset(page[:], 0.0)
+        ident = held([P, P], F32, "ident")
+        make_identity(nc, ident[:])
+        warm = held([P, 1], F32, "warm")
+        nc.scalar.activation(warm[:], ident[:, 0:1], ACT.Tanh)
+
+        offs_sb = held([P, S // 16], U16, "offs_sb")
+        offs2_sb = held([P, M // 16], U16, "offs2_sb")
+        offs3_sb = held([P, M // 16], U16, "offs3_sb")
+        tab_sb = held([P, T], I32, "tab_sb")
+        plume_raw = held([P, H // 2], I32, "plume_raw")
+        haz_sb = held([P, blocks, N], I32, "haz_sb")
+        wgt_sb = held([P, M], F32, "wgt_sb")
+        wgo_sb = held([P, M], F32, "wgo_sb")
+        shore_sb = held([P, blocks, PACK], F32, "shore_sb")
+        tide_sb = held([P, PACK, M], F32, "tide_sb")
+        raw = {}
+
+        def load_weight(name, w, b):
+            raw[name, b] = held([P, PACK, KP], F32, f"raw_{name}{b}")
+            nc.sync.dma_start(raw[name, b][:], w[:, b * KP:(b + 1) * KP].rearrange("(p j) c -> p j c", j=PACK))
+
+        nc.sync.dma_start(offs_sb[:], offs)
+        load_weight("foam", wfoam, 0)
+        load_scale_rows(tab_plane, tab_scales[0].bitcast(I32).rearrange("(q r) t -> r q t", r=4))
+        nc.sync.dma_start(plume_raw[:], wplume_words[0].bitcast(I32))
+        nc.sync.dma_start(tab_sb[:], tab_words[0].rearrange("p t i -> p (t i)").bitcast(I32))
+        load_scale_rows(plume_plane_raw, wplume_scales[0].bitcast(I32).rearrange("(q r) c -> r q c", r=4))
+        load_weight("view", wview, 0)
+        nc.sync.dma_start(offs2_sb[:], offs2)
+        nc.sync.dma_start(wgt_sb[:], wgt)
+        nc.sync.dma_start(shore_sb[:], shore.rearrange("(b p i) -> p b i", p=P, i=PACK))
+        load_weight("foam", wfoam, 1)
+        load_weight("view", wview, 1)
+        nc.sync.dma_start(tide_sb[:], tide.rearrange("(p i) m -> p i m", i=PACK))
+        nc.sync.dma_start(haz_sb[:], whaz_words.rearrange("a p c i -> p a (c i)").bitcast(I32))
+        haz_rows = whaz_scales.bitcast(I32).rearrange("a (q r) c -> r q a c", r=4)
+        for r in range(4):
+            nc.sync.dma_start(haz_plane[r:P:32, :].rearrange("q (a c) -> q a c", a=blocks), haz_rows[r])
+        nc.sync.dma_start(wgo_sb[:], wgo)
+        nc.sync.dma_start(offs3_sb[:], offs3)
+
+        codes, planes = {}, {}
+
+        def weave_weight(name, b, engine):
+            woven = ring.tile([P, PACK, P, PACK], BF16, name="woven", align_bytes=64)
+            dst = woven[:].rearrange("p i q j -> p q j i")
+            src = raw[name, b][:].rearrange("p j (q i) -> p q j i", i=PACK)
+            if engine == "vector":
+                nc.vector.tensor_copy(dst, src)
+            else:
+                nc.scalar.copy(dst, src)
+            return woven
+
+        def quantise_weight(name, b, woven):
+            codes[name, b] = held([P, KP], U32, f"codes_{name}{b}")
+            planes[name, b] = held([P, KP], U8, f"plane_{name}{b}")
+            nc.vector.quantize_mx(codes[name, b][:].bitcast(FP8X4), planes[name, b][:],
+                                  woven[:].rearrange("p i q j -> p (i q j)"))
+
+        woven_foam = weave_weight("foam", 0, "scalar")
+
+        v_plane = held([P, S], U8, "v_plane")
+        nc.vector.tensor_copy(v_plane[:], tab_plane[:].bitcast(U8).indirect(offs_sb[:]))
+        quantise_weight("foam", 0, woven_foam)
+
+        plume_codes = held([P, 2 * H], U8, "plume_codes")
+        plume_plane = held([P, H], U8, "plume_plane")
+        nc.vector.tensor_copy(plume_codes[:].bitcast(U16).rearrange("p (b i q) -> p b i q", b=blocks, i=PACK),
+                              plume_raw[:].bitcast(U16).rearrange("p (b q i) -> p b i q", b=blocks, i=PACK))
+        v_words = []
+        for half in range(S // BANK):
+            v_words.append(held([P, BANK], U32, f"v_words{half}"))
+            nc.vector.tensor_copy(v_words[half][:],
+                                  tab_sb[:].bitcast(U32).indirect(offs_sb[:, half * 32:(half + 1) * 32]))
+            if half == 0:
+                nc.vector.tensor_copy(plume_plane[:].rearrange("p (b i q) -> p b i q", b=blocks, i=PACK),
+                                      plume_plane_raw[:].bitcast(U8).rearrange("p (b q i) -> p b i q", b=blocks, i=PACK))
+
+        def product(tag, bufs, lhs, lhs_plane, half):
+            bank = psum.tile([P, BANK], F32, name=tag, tag=tag, bufs=bufs)
+            nc.tensor.matmul_mx(bank[:], lhsT=lhs, lhsT_scale=lhs_plane, rhs=v_words[half][:].bitcast(FP8X4),
+                                rhs_scale=v_plane[:, half * BANK:(half + 1) * BANK], start=True, stop=True)
+            return bank
+
+        h_tiles = {}
+
+        def stronger(b, i):
+            h_tiles[b, i] = held([P, S], F32, f"h{b}{i}")
+            col = b * KP + i * P
+            for half in range(S // BANK):
+                plume = product("left", 2, plume_codes[:, 2 * col:2 * (col + P)].bitcast(FP4X4),
+                                plume_plane[:, col:col + P], half)
+                foam = product("mid", 3, codes["foam", b][:, i * P:(i + 1) * P].bitcast(FP8X4),
+                               planes["foam", b][:, i * P:(i + 1) * P], half)
+                plume_sb = ring.tile([P, BANK], F32, name="plume_sb", bufs=3)
+                nc.scalar.copy(plume_sb[:], plume[:])
+                nc.vector.tensor_tensor(h_tiles[b, i][:, half * BANK:(half + 1) * BANK], foam[:], plume_sb[:], ALU.max)
+
+        def capped(b, i):
+            for half in range(S // BANK):
+                view = product("right", 3, codes["view", b][:, i * P:(i + 1) * P].bitcast(FP8X4),
+                               planes["view", b][:, i * P:(i + 1) * P], half)
+                cols = h_tiles[b, i][:, half * BANK:(half + 1) * BANK]
+                nc.vector.tensor_tensor(cols, view[:], cols, ALU.min)
+
+        x_rows = {(b, u): held([P, PACK, HALF], BF16, f"x_rows{b}{u}") for b in range(blocks) for u in range(2)}
+        x_codes, x_planes = {}, {}
+
+        def pick(b, i, u):
+            picked = ring.tile([P, HALF], F32, name="picked", bufs=4)
+            nc.vector.tensor_tensor(picked[:], h_tiles[b, i][:].indirect(offs2_sb[:, u * OFFS_COLS:(u + 1) * OFFS_COLS]),
+                                    wgt_sb[:, u * HALF:(u + 1) * HALF], ALU.mult)
+            nc.scalar.activation(x_rows[b, u][:, i, :], picked[:], ACT.Identity, bias=shore_sb[:, b, i:i + 1])
+
+        def weave_x(b, u):
+            woven = ring.tile([P, HALF, PACK], BF16, name="woven_x", align_bytes=64)
+            nc.scalar.copy(woven[:].rearrange("p (c k) t -> p c t k", k=4),
+                           x_rows[b, u][:].rearrange("p t (c k) -> p c t k", k=4))
+            return woven
+
+        def quantise_x(b, u, woven):
+            x_codes[b, u] = held([P, HALF], U32, f"x_codes{b}{u}")
+            x_planes[b, u] = held([P, HALF], U8, f"x_plane{b}{u}")
+            nc.vector.quantize_mx(x_codes[b, u][:].bitcast(FP8X4), x_planes[b, u][:],
+                                  woven[:].rearrange("p m t -> p (m t)"))
+
+        tide_t = []
+
+        def turn_tide(c):
+            bank = psum.tile([P, BANK], F32, name="left", tag="left", bufs=2)
+            for i in range(PACK):
+                nc.tensor.transpose(bank[:, i * P:(i + 1) * P], tide_sb[:, i, c * P:(c + 1) * P], ident[:])
+            tide_t.append(held([P, BANK], F32, f"tide_t{c}"))
+            nc.scalar.copy(tide_t[c][:], bank[:])
+
+        y_tiles = [held([P, PACK, HALF], F32, f"y{u}") for u in range(2)]
+
+        def score(u, c):
+            cols = slice(c * P, (c + 1) * P)
+            q = psum.tile([P, BANK], F32, name="mid", tag="mid", bufs=3)
+            for b in range(blocks):
+                nc.tensor.matmul_mx(q[:], lhsT=x_codes[b, u][:, cols].bitcast(FP8X4), lhsT_scale=x_planes[b, u][:, cols],
+                                    rhs=haz_sb[:, b, :].bitcast(FP8X4), rhs_scale=haz_plane[:, b * N // 4:(b + 1) * N // 4].bitcast(U8),
+                                    start=(b == 0), stop=(b == blocks - 1))
+            dealt = q[:].rearrange("m (p i) -> m i p", i=PACK)
+            tanh_q = ring.tile([P, PACK, P], F32, name="tanh_q")
+            nc.scalar.activation(tanh_q[:], dealt, ACT.Tanh)
+            q_tide = ring.tile([P, PACK, P], F32, name="q_tide")
+            nc.vector.tensor_tensor(q_tide[:], dealt, tide_t[2 * u + c][:].rearrange("m (i p) -> m i p", i=PACK), ALU.mult)
+            return q_tide, tanh_q
+
+        def add_turned(u, c, terms):
+            bank = psum.tile([P, BANK], F32, name="right", tag="right", bufs=3)
+            for i in range(PACK):
+                for n, term in enumerate(terms):
+                    nc.tensor.matmul(bank[:, i * P:(i + 1) * P], lhsT=term[:, i, :], rhs=ident[:], is_transpose=True,
+                                     start=(n == 0), stop=(n == len(terms) - 1))
+            nc.scalar.copy(y_tiles[u][:, :, c * P:(c + 1) * P], bank[:].rearrange("p (i m) -> p i m", i=PACK))
+
+        def place(i, u):
+            nc.vector.tensor_tensor(pages[i][:].indirect(offs3_sb[:, u * OFFS_COLS:(u + 1) * OFFS_COLS]),
+                                    y_tiles[u][:, i, :], wgo_sb[:, u * HALF:(u + 1) * HALF], ALU.mult)
+
+        def finish(u):
+            terms = [score(u, c) for c in range(2)]
+            for c in range(2):
+                add_turned(u, c, terms[c])
+
+        stronger(0, 0)
+        stronger(0, 1)
+        quantise_weight("view", 0, weave_weight("view", 0, "vector"))
+        stronger(0, 2)
+        stronger(0, 3)
+        woven_foam = weave_weight("foam", 1, "scalar")
+        capped(0, 0)
+        for i in range(1, PACK):
+            capped(0, i)
+            pick(0, i - 1, 0)
+            if i == 1:
+                quantise_weight("foam", 1, woven_foam)
+                woven_view = weave_weight("view", 1, "scalar")
+        quantise_weight("view", 1, woven_view)
+        stronger(1, 0)
+        pick(0, PACK - 1, 0)
+        woven = weave_x(0, 0)
+        for i in range(PACK):
+            capped(1, i)
+            if i == 0:
+                quantise_x(0, 0, woven)
+            if i + 1 < PACK:
+                stronger(1, i + 1)
+            else:
+                pick(0, 0, 1)
+            pick(1, i, 0)
+            turn_tide(i)
+        woven = weave_x(1, 0)
+        pick(0, 1, 1)
+        pick(0, 2, 1)
+        quantise_x(1, 0, woven)
+        pick(0, 3, 1)
+        woven = weave_x(0, 1)
+        finish(0)
+        for i in range(PACK):
+            pick(1, i, 1)
+        quantise_x(0, 1, woven)
+        woven = weave_x(1, 1)
+        place(0, 0)
+        quantise_x(1, 1, woven)
+        finish(1)
+        for i in range(1, PACK):
+            place(i, 0)
+        rows = out.rearrange("(p i) t -> p i t", i=PACK)
+        for i in range(PACK):
+            place(i, 1)
+            nc.sync.dma_start(rows[:, i, :], pages[i][:])

@@ -38,9 +38,9 @@ def tile_list_rip_current_watch_kernel(tc, tab_words, tab_scales, offs, wfoam, w
         def held(shape, dtype, name):
             return keep.tile(shape, dtype, name=name, align_bytes=64)
 
-        def load_scale_rows(plane, rows):
+        def load_scale_rows(queue, plane, rows):
             for r in range(4):
-                nc.sync.dma_start(plane[r:P:32, :], rows[r])
+                queue.dma_start(plane[r:P:32, :], rows[r])
 
         tab_plane = held([P, T // 4], I32, "tab_plane")
         plume_plane_raw = held([P, H // 4], I32, "plume_plane_raw")
@@ -49,7 +49,7 @@ def tile_list_rip_current_watch_kernel(tc, tab_words, tab_scales, offs, wfoam, w
         for plane in (tab_plane, plume_plane_raw, haz_plane):
             nc.vector.memset(plane[:], 0)
         for page in pages:
-            nc.vector.memset(page[:], 0.0)
+            nc.vector.memset(page[:].bitcast(I32), 0)
         ident = held([P, P], F32, "ident")
         make_identity(nc, ident[:])
         warm = held([P, 1], F32, "warm")
@@ -67,17 +67,20 @@ def tile_list_rip_current_watch_kernel(tc, tab_words, tab_scales, offs, wfoam, w
         tide_sb = held([P, PACK, M], F32, "tide_sb")
         raw = {}
 
-        def load_weight(name, w, b):
-            raw[name, b] = held([P, PACK, KP], F32, f"raw_{name}{b}")
-            nc.sync.dma_start(raw[name, b][:], w[:, b * KP:(b + 1) * KP].rearrange("(p j) c -> p j c", j=PACK))
+        def load_weight(name, w, b, pieces=1):
+            width = KP // pieces
+            raw[name, b] = [held([P, PACK, width], F32, f"raw_{name}{b}{n}") for n in range(pieces)]
+            for n in range(pieces):
+                cols = slice(b * KP + n * width, b * KP + (n + 1) * width)
+                nc.sync.dma_start(raw[name, b][n][:], w[:, cols].rearrange("(p j) c -> p j c", j=PACK))
 
         nc.sync.dma_start(offs_sb[:], offs)
         load_weight("foam", wfoam, 0)
-        load_scale_rows(tab_plane, tab_scales[0].bitcast(I32).rearrange("(q r) t -> r q t", r=4))
+        load_scale_rows(nc.sync, tab_plane, tab_scales[0].bitcast(I32).rearrange("(q r) t -> r q t", r=4))
         nc.sync.dma_start(plume_raw[:], wplume_words[0].bitcast(I32))
         nc.sync.dma_start(tab_sb[:], tab_words[0].rearrange("p t i -> p (t i)").bitcast(I32))
-        load_scale_rows(plume_plane_raw, wplume_scales[0].bitcast(I32).rearrange("(q r) c -> r q c", r=4))
-        load_weight("view", wview, 0)
+        load_scale_rows(nc.sync, plume_plane_raw, wplume_scales[0].bitcast(I32).rearrange("(q r) c -> r q c", r=4))
+        load_weight("view", wview, 0, pieces=2)
         nc.sync.dma_start(offs2_sb[:], offs2)
         nc.sync.dma_start(wgt_sb[:], wgt)
         nc.sync.dma_start(shore_sb[:], shore.rearrange("(b p i) -> p b i", p=P, i=PACK))
@@ -94,31 +97,35 @@ def tile_list_rip_current_watch_kernel(tc, tab_words, tab_scales, offs, wfoam, w
         codes, planes = {}, {}
 
         def weave_weight(name, b, engine):
-            woven = ring.tile([P, PACK, P, PACK], BF16, name="woven", align_bytes=64)
-            dst = woven[:].rearrange("p i q j -> p q j i")
-            src = raw[name, b][:].rearrange("p j (q i) -> p q j i", i=PACK)
-            if engine == "vector":
-                nc.vector.tensor_copy(dst, src)
-            else:
-                nc.scalar.copy(dst, src)
+            woven = held([P, PACK, P, PACK], BF16, f"woven_{name}{b}")
+            share = P // len(raw[name, b])
+            for n, piece in enumerate(raw[name, b]):
+                dst = woven[:, :, n * share:(n + 1) * share, :]
+                if engine == "gpsimd":
+                    nc.gpsimd.tensor_scalar(dst, piece[:].rearrange("p j (q i) -> p i q j", i=PACK), 1.0, 0.0,
+                                            ALU.mult, ALU.add)
+                else:
+                    nc.scalar.copy(dst.rearrange("p i q j -> p q j i"), piece[:].rearrange("p j (q i) -> p q j i", i=PACK))
             return woven
 
-        def quantise_weight(name, b, woven):
+        def quantise_weight(name, b, woven, pieces=1):
             codes[name, b] = held([P, KP], U32, f"codes_{name}{b}")
             planes[name, b] = held([P, KP], U8, f"plane_{name}{b}")
-            nc.vector.quantize_mx(codes[name, b][:].bitcast(FP8X4), planes[name, b][:],
-                                  woven[:].rearrange("p i q j -> p (i q j)"))
+            width = KP // pieces
+            flat = woven[:].rearrange("p i q j -> p (i q j)")
+            for n in range(pieces):
+                cols = slice(n * width, (n + 1) * width)
+                nc.vector.quantize_mx(codes[name, b][:, cols].bitcast(FP8X4), planes[name, b][:, cols],
+                                      flat[:, n * width * PACK:(n + 1) * width * PACK])
 
         woven_foam = weave_weight("foam", 0, "scalar")
-
         v_plane = held([P, S], U8, "v_plane")
         nc.vector.tensor_copy(v_plane[:], tab_plane[:].bitcast(U8).indirect(offs_sb[:]))
-        quantise_weight("foam", 0, woven_foam)
-
         plume_codes = held([P, 2 * H], U8, "plume_codes")
         plume_plane = held([P, H], U8, "plume_plane")
         nc.vector.tensor_copy(plume_codes[:].bitcast(U16).rearrange("p (b i q) -> p b i q", b=blocks, i=PACK),
                               plume_raw[:].bitcast(U16).rearrange("p (b q i) -> p b i q", b=blocks, i=PACK))
+        quantise_weight("foam", 0, woven_foam)
         v_words = []
         for half in range(S // BANK):
             v_words.append(held([P, BANK], U32, f"v_words{half}"))
@@ -136,17 +143,20 @@ def tile_list_rip_current_watch_kernel(tc, tab_words, tab_scales, offs, wfoam, w
 
         h_tiles = {}
 
-        def stronger(b, i):
+        def plume_sign(b, i):
             h_tiles[b, i] = held([P, S], F32, f"h{b}{i}")
             col = b * KP + i * P
             for half in range(S // BANK):
                 plume = product("left", 2, plume_codes[:, 2 * col:2 * (col + P)].bitcast(FP4X4),
                                 plume_plane[:, col:col + P], half)
+                nc.scalar.copy(h_tiles[b, i][:, half * BANK:(half + 1) * BANK], plume[:])
+
+        def stronger(b, i):
+            for half in range(S // BANK):
                 foam = product("mid", 3, codes["foam", b][:, i * P:(i + 1) * P].bitcast(FP8X4),
                                planes["foam", b][:, i * P:(i + 1) * P], half)
-                plume_sb = ring.tile([P, BANK], F32, name="plume_sb", bufs=3)
-                nc.scalar.copy(plume_sb[:], plume[:])
-                nc.vector.tensor_tensor(h_tiles[b, i][:, half * BANK:(half + 1) * BANK], foam[:], plume_sb[:], ALU.max)
+                cols = h_tiles[b, i][:, half * BANK:(half + 1) * BANK]
+                nc.vector.tensor_tensor(cols, foam[:], cols, ALU.max)
 
         def capped(b, i):
             for half in range(S // BANK):
@@ -158,23 +168,29 @@ def tile_list_rip_current_watch_kernel(tc, tab_words, tab_scales, offs, wfoam, w
         x_rows = {(b, u): held([P, PACK, HALF], BF16, f"x_rows{b}{u}") for b in range(blocks) for u in range(2)}
         x_codes, x_planes = {}, {}
 
-        def pick(b, i, u):
-            picked = ring.tile([P, HALF], F32, name="picked", bufs=4)
-            nc.vector.tensor_tensor(picked[:], h_tiles[b, i][:].indirect(offs2_sb[:, u * OFFS_COLS:(u + 1) * OFFS_COLS]),
-                                    wgt_sb[:, u * HALF:(u + 1) * HALF], ALU.mult)
-            nc.scalar.activation(x_rows[b, u][:, i, :], picked[:], ACT.Identity, bias=shore_sb[:, b, i:i + 1])
+        def pick(b, i, u, picked):
+            window = h_tiles[b, i][:].indirect(offs2_sb[:, u * OFFS_COLS:(u + 1) * OFFS_COLS])
+            nc.vector.tensor_tensor(picked, window, wgt_sb[:, u * HALF:(u + 1) * HALF], ALU.mult)
+            nc.scalar.activation(x_rows[b, u][:, i, :], picked, ACT.Identity, bias=shore_sb[:, b, i:i + 1])
 
-        def weave_x(b, u):
-            woven = ring.tile([P, HALF, PACK], BF16, name="woven_x", align_bytes=64)
+        def pick_early(b, i):
+            picked = ring.tile([P, HALF], F32, name="picked", bufs=4)
+            pick(b, i, 0, picked[:])
+
+        def weave_x(b, first, chunks):
+            u, start, width = first // 2, first % 2 * P, chunks * P
+            woven = held([P, width, PACK], BF16, f"woven_x{b}{first}")
             nc.scalar.copy(woven[:].rearrange("p (c k) t -> p c t k", k=4),
-                           x_rows[b, u][:].rearrange("p t (c k) -> p c t k", k=4))
+                           x_rows[b, u][:, :, start:start + width].rearrange("p t (c k) -> p c t k", k=4))
             return woven
 
-        def quantise_x(b, u, woven):
-            x_codes[b, u] = held([P, HALF], U32, f"x_codes{b}{u}")
-            x_planes[b, u] = held([P, HALF], U8, f"x_plane{b}{u}")
-            nc.vector.quantize_mx(x_codes[b, u][:].bitcast(FP8X4), x_planes[b, u][:],
-                                  woven[:].rearrange("p m t -> p (m t)"))
+        def quantise_x(b, first, chunks, woven):
+            words = held([P, chunks * P], U32, f"x_codes{b}{first}")
+            plane = held([P, chunks * P], U8, f"x_plane{b}{first}")
+            nc.vector.quantize_mx(words[:].bitcast(FP8X4), plane[:], woven[:].rearrange("p m t -> p (m t)"))
+            for n in range(chunks):
+                x_codes[b, first + n] = words[:, n * P:(n + 1) * P]
+                x_planes[b, first + n] = plane[:, n * P:(n + 1) * P]
 
         tide_t = []
 
@@ -185,82 +201,111 @@ def tile_list_rip_current_watch_kernel(tc, tab_words, tab_scales, offs, wfoam, w
             tide_t.append(held([P, BANK], F32, f"tide_t{c}"))
             nc.scalar.copy(tide_t[c][:], bank[:])
 
-        y_tiles = [held([P, PACK, HALF], F32, f"y{u}") for u in range(2)]
+        y_rows, y_banks = {}, {}
 
-        def score(u, c):
-            cols = slice(c * P, (c + 1) * P)
-            q = psum.tile([P, BANK], F32, name="mid", tag="mid", bufs=3)
-            for b in range(blocks):
-                nc.tensor.matmul_mx(q[:], lhsT=x_codes[b, u][:, cols].bitcast(FP8X4), lhsT_scale=x_planes[b, u][:, cols],
-                                    rhs=haz_sb[:, b, :].bitcast(FP8X4), rhs_scale=haz_plane[:, b * N // 4:(b + 1) * N // 4].bitcast(U8),
-                                    start=(b == 0), stop=(b == blocks - 1))
-            dealt = q[:].rearrange("m (p i) -> m i p", i=PACK)
+        def make_y(u, first, count, tag):
+            rows = keep.tile([P, count, HALF], F32, name=f"y{u}{first}", tag=tag, align_bytes=64)
+            for c in range(2):
+                bank = y_banks[2 * u + c][:].rearrange("p (i m) -> p i m", i=PACK)
+                nc.scalar.copy(rows[:, :, c * P:(c + 1) * P], bank[:, first:first + count, :])
+            for n in range(count):
+                y_rows[first + n, u] = rows[:, n, :]
+
+        q_banks = {}
+
+        def hazard_pass(b, c):
+            if b == 0:
+                tag, bufs = ("left", 2) if c < 2 else ("mid", 3)
+                q_banks[c] = psum.tile([P, BANK], F32, name=tag, tag=tag, bufs=bufs)
+            nc.tensor.matmul_mx(q_banks[c][:], lhsT=x_codes[b, c].bitcast(FP8X4), lhsT_scale=x_planes[b, c],
+                                rhs=haz_sb[:, b, :].bitcast(FP8X4),
+                                rhs_scale=haz_plane[:, b * N // 4:(b + 1) * N // 4].bitcast(U8),
+                                start=(b == 0), stop=(b == blocks - 1))
+
+        def score(c):
+            dealt = q_banks[c][:].rearrange("m (p i) -> m i p", i=PACK)
             tanh_q = ring.tile([P, PACK, P], F32, name="tanh_q")
             nc.scalar.activation(tanh_q[:], dealt, ACT.Tanh)
             q_tide = ring.tile([P, PACK, P], F32, name="q_tide")
-            nc.vector.tensor_tensor(q_tide[:], dealt, tide_t[2 * u + c][:].rearrange("m (i p) -> m i p", i=PACK), ALU.mult)
-            return q_tide, tanh_q
+            nc.vector.tensor_tensor(q_tide[:], dealt, tide_t[c][:].rearrange("m (i p) -> m i p", i=PACK), ALU.mult)
+            return tanh_q, q_tide
 
-        def add_turned(u, c, terms):
+        def add_turned(c, terms):
             bank = psum.tile([P, BANK], F32, name="right", tag="right", bufs=3)
             for i in range(PACK):
                 for n, term in enumerate(terms):
                     nc.tensor.matmul(bank[:, i * P:(i + 1) * P], lhsT=term[:, i, :], rhs=ident[:], is_transpose=True,
-                                     start=(n == 0), stop=(n == len(terms) - 1))
-            nc.scalar.copy(y_tiles[u][:, :, c * P:(c + 1) * P], bank[:].rearrange("p (i m) -> p i m", i=PACK))
+                                     start=(n == 0), stop=(n == 1))
+            y_banks[c] = bank
 
         def place(i, u):
             nc.vector.tensor_tensor(pages[i][:].indirect(offs3_sb[:, u * OFFS_COLS:(u + 1) * OFFS_COLS]),
-                                    y_tiles[u][:, i, :], wgo_sb[:, u * HALF:(u + 1) * HALF], ALU.mult)
+                                    y_rows[i, u], wgo_sb[:, u * HALF:(u + 1) * HALF], ALU.mult)
 
-        def finish(u):
-            terms = [score(u, c) for c in range(2)]
-            for c in range(2):
-                add_turned(u, c, terms[c])
-
-        stronger(0, 0)
-        stronger(0, 1)
-        quantise_weight("view", 0, weave_weight("view", 0, "vector"))
-        stronger(0, 2)
-        stronger(0, 3)
+        for i in range(PACK):
+            plume_sign(0, i)
+            stronger(0, i)
+        quantise_weight("view", 0, weave_weight("view", 0, "gpsimd"), pieces=2)
         woven_foam = weave_weight("foam", 1, "scalar")
         capped(0, 0)
         for i in range(1, PACK):
             capped(0, i)
-            pick(0, i - 1, 0)
+            pick_early(0, i - 1)
             if i == 1:
                 quantise_weight("foam", 1, woven_foam)
+                plume_sign(1, 0)
                 woven_view = weave_weight("view", 1, "scalar")
-        quantise_weight("view", 1, woven_view)
+            plume_sign(1, i)
         stronger(1, 0)
-        pick(0, PACK - 1, 0)
-        woven = weave_x(0, 0)
+        pick_early(0, PACK - 1)
+        quantise_weight("view", 1, woven_view)
+        woven = weave_x(0, 0, 2)
         for i in range(PACK):
-            capped(1, i)
-            if i == 0:
-                quantise_x(0, 0, woven)
             if i + 1 < PACK:
                 stronger(1, i + 1)
+            capped(1, i)
+            if i == 0:
+                quantise_x(0, 0, 2, woven)
             else:
-                pick(0, 0, 1)
-            pick(1, i, 0)
+                pick_early(1, i - 1)
             turn_tide(i)
-        woven = weave_x(1, 0)
-        pick(0, 1, 1)
-        pick(0, 2, 1)
-        quantise_x(1, 0, woven)
-        pick(0, 3, 1)
-        woven = weave_x(0, 1)
-        finish(0)
-        for i in range(PACK):
-            pick(1, i, 1)
-        quantise_x(0, 1, woven)
-        woven = weave_x(1, 1)
+        pick_early(1, PACK - 1)
+        late = [(b, i) for b in range(blocks) for i in range(PACK)]
+        first_late = keep.tile([P, 5, HALF], F32, name="first_late", tag="codes_view1", align_bytes=64)
+        woven = [weave_x(1, c, 1) for c in range(2)]
+        for c in range(2):
+            hazard_pass(0, c)
+        pick(*late[0], 1, first_late[:, 0, :])
+        for c in range(2):
+            pick(*late[1 + c], 1, first_late[:, 1 + c, :])
+            quantise_x(1, c, 1, woven[c])
+            hazard_pass(1, c)
+        for n in range(3, 5):
+            pick(*late[n], 1, first_late[:, n, :])
+        for c in range(2):
+            add_turned(c, score(c))
+        make_y(0, 0, 2, "y_first")
+        woven_first = weave_x(0, 2, 2)
+        last_late = keep.tile([P, 3, HALF], F32, name="last_late", tag="tide_t0", align_bytes=64)
+        for n in range(5, 8):
+            pick(*late[n], 1, last_late[:, n - 5, :])
+        woven = [weave_x(1, c, 1) for c in range(2, 4)]
+        quantise_x(0, 2, 2, woven_first)
+        for c in range(2, 4):
+            hazard_pass(0, c)
         place(0, 0)
-        quantise_x(1, 1, woven)
-        finish(1)
-        for i in range(1, PACK):
-            place(i, 0)
+        place(1, 0)
+        for c in range(2, 4):
+            quantise_x(1, c, 1, woven[c - 2])
+            hazard_pass(1, c)
+        make_y(0, 2, 1, "x_rows11")
+        place(2, 0)
+        terms = [score(c) for c in range(2, 4)]
+        make_y(0, 3, 1, "x_codes13")
+        for c in range(2, 4):
+            add_turned(c, terms[c - 2])
+        place(3, 0)
+        make_y(1, 0, PACK, "y_last")
         rows = out.rearrange("(p i) t -> p i t", i=PACK)
         for i in range(PACK):
             place(i, 1)

from contextlib import ExitStack

import concourse.mybir as mybir
from concourse.masks import make_identity

K, T, S, H, M, T2, N = 512, 4096, 1024, 1024, 512, 1024, 512
FLOPS = 2 * (3 * K * H * S + H * N * M)

F32 = mybir.dt.float32
BF16 = mybir.dt.bfloat16
I32 = mybir.dt.int32
U32 = mybir.dt.uint32
U16 = mybir.dt.uint16
U8 = mybir.dt.uint8
FP8X4 = mybir.dt.float8_e4m3fn_x4
FP4X4 = mybir.dt.float4_e2m1fn_x4
ALU = mybir.AluOpType
ACT = mybir.ActivationFunctionType

P = 128
PACK = 4
KP = P * PACK
BANK = 512
HALF = M // 2
OFFS_COLS = HALF // 16


def tile_list_rip_current_watch_kernel(tc, tab_words, tab_scales, offs, wfoam, wplume_words, wplume_scales,
                                                 wview, offs2, wgt, shore, whaz_words, whaz_scales, tide, offs3, wgo,
                                                 out):
    nc = tc.nc
    blocks = H // KP
    with ExitStack() as ctx:
        keep = ctx.enter_context(tc.tile_pool(name="keep", bufs=1))
        ring = ctx.enter_context(tc.tile_pool(name="ring", bufs=2))
        psum = ctx.enter_context(tc.psum_pool(name="psum", bufs=1))

        def held(shape, dtype, name):
            return keep.tile(shape, dtype, name=name, align_bytes=64)

        def load_scale_rows(queue, plane, rows):
            for r in range(4):
                queue.dma_start(plane[r:P:32, :], rows[r])

        tab_plane = held([P, T // 4], I32, "tab_plane")
        plume_plane_raw = held([P, H // 4], I32, "plume_plane_raw")
        haz_plane = held([P, blocks * N // 4], I32, "haz_plane")
        pages = [held([P, T2], F32, f"page{i}") for i in range(PACK)]
        for plane in (tab_plane, plume_plane_raw, haz_plane):
            nc.vector.memset(plane[:], 0)
        for page in pages:
            nc.vector.memset(page[:].bitcast(I32), 0)
        ident = held([P, P], F32, "ident")
        make_identity(nc, ident[:])
        warm = held([P, 1], F32, "warm")
        nc.scalar.activation(warm[:], ident[:, 0:1], ACT.Tanh)

        offs_sb = held([P, S // 16], U16, "offs_sb")
        offs2_sb = held([P, M // 16], U16, "offs2_sb")
        offs3_sb = held([P, M // 16], U16, "offs3_sb")
        tab_sb = held([P, T], I32, "tab_sb")
        plume_raw = held([P, H // 2], I32, "plume_raw")
        haz_sb = held([P, blocks, N], I32, "haz_sb")
        wgt_sb = held([P, M], F32, "wgt_sb")
        wgo_sb = held([P, M], F32, "wgo_sb")
        shore_sb = held([P, blocks, PACK], F32, "shore_sb")
        tide_sb = held([P, PACK, M], F32, "tide_sb")
        raw = {}

        def load_weight(name, w, b, pieces=1):
            width = KP // pieces
            raw[name, b] = [held([P, PACK, width], F32, f"raw_{name}{b}{n}") for n in range(pieces)]
            for n in range(pieces):
                cols = slice(b * KP + n * width, b * KP + (n + 1) * width)
                nc.sync.dma_start(raw[name, b][n][:], w[:, cols].rearrange("(p j) c -> p j c", j=PACK))

        nc.sync.dma_start(offs_sb[:], offs)
        load_weight("foam", wfoam, 0)
        load_scale_rows(nc.sync, tab_plane, tab_scales[0].bitcast(I32).rearrange("(q r) t -> r q t", r=4))
        nc.sync.dma_start(plume_raw[:], wplume_words[0].bitcast(I32))
        nc.sync.dma_start(tab_sb[:], tab_words[0].rearrange("p t i -> p (t i)").bitcast(I32))
        load_scale_rows(nc.sync, plume_plane_raw, wplume_scales[0].bitcast(I32).rearrange("(q r) c -> r q c", r=4))
        load_weight("view", wview, 0, pieces=2)
        nc.sync.dma_start(offs2_sb[:], offs2)
        nc.sync.dma_start(wgt_sb[:], wgt)
        nc.sync.dma_start(shore_sb[:], shore.rearrange("(b p i) -> p b i", p=P, i=PACK))
        load_weight("foam", wfoam, 1)
        load_weight("view", wview, 1)
        nc.sync.dma_start(tide_sb[:], tide.rearrange("(p i) m -> p i m", i=PACK))
        nc.sync.dma_start(haz_sb[:], whaz_words.rearrange("a p c i -> p a (c i)").bitcast(I32))
        haz_rows = whaz_scales.bitcast(I32).rearrange("a (q r) c -> r q a c", r=4)
        for r in range(4):
            nc.sync.dma_start(haz_plane[r:P:32, :].rearrange("q (a c) -> q a c", a=blocks), haz_rows[r])
        nc.sync.dma_start(wgo_sb[:], wgo)
        nc.sync.dma_start(offs3_sb[:], offs3)

        codes, planes = {}, {}

        def weave_weight(name, b, engine):
            woven = held([P, PACK, P, PACK], BF16, f"woven_{name}{b}")
            share = P // len(raw[name, b])
            for n, piece in enumerate(raw[name, b]):
                dst = woven[:, :, n * share:(n + 1) * share, :]
                if engine == "gpsimd":
                    nc.gpsimd.tensor_scalar(dst, piece[:].rearrange("p j (q i) -> p i q j", i=PACK), 1.0, 0.0,
                                            ALU.mult, ALU.add)
                else:
                    nc.scalar.copy(dst.rearrange("p i q j -> p q j i"), piece[:].rearrange("p j (q i) -> p q j i", i=PACK))
            return woven

        def quantise_weight(name, b, woven, pieces=1):
            codes[name, b] = held([P, KP], U32, f"codes_{name}{b}")
            planes[name, b] = held([P, KP], U8, f"plane_{name}{b}")
            width = KP // pieces
            flat = woven[:].rearrange("p i q j -> p (i q j)")
            for n in range(pieces):
                cols = slice(n * width, (n + 1) * width)
                nc.vector.quantize_mx(codes[name, b][:, cols].bitcast(FP8X4), planes[name, b][:, cols],
                                      flat[:, n * width * PACK:(n + 1) * width * PACK])

        woven_foam = weave_weight("foam", 0, "scalar")
        v_plane = held([P, S], U8, "v_plane")
        nc.vector.tensor_copy(v_plane[:], tab_plane[:].bitcast(U8).indirect(offs_sb[:]))
        plume_codes = held([P, 2 * H], U8, "plume_codes")
        plume_plane = held([P, H], U8, "plume_plane")
        nc.vector.tensor_copy(plume_codes[:].bitcast(U16).rearrange("p (b i q) -> p b i q", b=blocks, i=PACK),
                              plume_raw[:].bitcast(U16).rearrange("p (b q i) -> p b i q", b=blocks, i=PACK))
        quantise_weight("foam", 0, woven_foam)
        v_words = []
        for half in range(S // BANK):
            v_words.append(held([P, BANK], U32, f"v_words{half}"))
            nc.vector.tensor_copy(v_words[half][:],
                                  tab_sb[:].bitcast(U32).indirect(offs_sb[:, half * 32:(half + 1) * 32]))
            if half == 0:
                nc.vector.tensor_copy(plume_plane[:].rearrange("p (b i q) -> p b i q", b=blocks, i=PACK),
                                      plume_plane_raw[:].bitcast(U8).rearrange("p (b q i) -> p b i q", b=blocks, i=PACK))

        def product(tag, bufs, lhs, lhs_plane, half):
            bank = psum.tile([P, BANK], F32, name=tag, tag=tag, bufs=bufs)
            nc.tensor.matmul_mx(bank[:], lhsT=lhs, lhsT_scale=lhs_plane, rhs=v_words[half][:].bitcast(FP8X4),
                                rhs_scale=v_plane[:, half * BANK:(half + 1) * BANK], start=True, stop=True)
            return bank

        h_tiles = {}

        def plume_sign(b, i):
            h_tiles[b, i] = held([P, S], F32, f"h{b}{i}")
            col = b * KP + i * P
            for half in range(S // BANK):
                plume = product("left", 2, plume_codes[:, 2 * col:2 * (col + P)].bitcast(FP4X4),
                                plume_plane[:, col:col + P], half)
                nc.scalar.copy(h_tiles[b, i][:, half * BANK:(half + 1) * BANK], plume[:])

        def stronger(b, i):
            for half in range(S // BANK):
                foam = product("mid", 3, codes["foam", b][:, i * P:(i + 1) * P].bitcast(FP8X4),
                               planes["foam", b][:, i * P:(i + 1) * P], half)
                cols = h_tiles[b, i][:, half * BANK:(half + 1) * BANK]
                nc.vector.tensor_tensor(cols, foam[:], cols, ALU.max)

        def capped(b, i):
            for half in range(S // BANK):
                view = product("right", 3, codes["view", b][:, i * P:(i + 1) * P].bitcast(FP8X4),
                               planes["view", b][:, i * P:(i + 1) * P], half)
                cols = h_tiles[b, i][:, half * BANK:(half + 1) * BANK]
                nc.vector.tensor_tensor(cols, view[:], cols, ALU.min)

        x_rows = {(b, u): held([P, PACK, HALF], BF16, f"x_rows{b}{u}") for b in range(blocks) for u in range(2)}
        x_codes, x_planes = {}, {}

        def pick(b, i, u, picked):
            window = h_tiles[b, i][:].indirect(offs2_sb[:, u * OFFS_COLS:(u + 1) * OFFS_COLS])
            nc.vector.tensor_tensor(picked, window, wgt_sb[:, u * HALF:(u + 1) * HALF], ALU.mult)
            nc.scalar.activation(x_rows[b, u][:, i, :], picked, ACT.Identity, bias=shore_sb[:, b, i:i + 1])

        def pick_early(b, i):
            picked = ring.tile([P, HALF], F32, name="picked", bufs=4)
            pick(b, i, 0, picked[:])

        def weave_x(b, first, chunks):
            u, start, width = first // 2, first % 2 * P, chunks * P
            woven = held([P, width, PACK], BF16, f"woven_x{b}{first}")
            nc.scalar.copy(woven[:].rearrange("p (c k) t -> p c t k", k=4),
                           x_rows[b, u][:, :, start:start + width].rearrange("p t (c k) -> p c t k", k=4))
            return woven

        def quantise_x(b, first, chunks, woven):
            words = held([P, chunks * P], U32, f"x_codes{b}{first}")
            plane = held([P, chunks * P], U8, f"x_plane{b}{first}")
            nc.vector.quantize_mx(words[:].bitcast(FP8X4), plane[:], woven[:].rearrange("p m t -> p (m t)"))
            for n in range(chunks):
                x_codes[b, first + n] = words[:, n * P:(n + 1) * P]
                x_planes[b, first + n] = plane[:, n * P:(n + 1) * P]

        tide_t = []

        def turn_tide(c):
            bank = psum.tile([P, BANK], F32, name="left", tag="left", bufs=2)
            for i in range(PACK):
                nc.tensor.transpose(bank[:, i * P:(i + 1) * P], tide_sb[:, i, c * P:(c + 1) * P], ident[:])
            tide_t.append(held([P, BANK], F32, f"tide_t{c}"))
            nc.scalar.copy(tide_t[c][:], bank[:])

        y_rows, y_banks = {}, {}

        def make_y(u, first, count, tag):
            rows = keep.tile([P, count, HALF], F32, name=f"y{u}{first}", tag=tag, align_bytes=64)
            for c in range(2):
                bank = y_banks[2 * u + c][:].rearrange("p (i m) -> p i m", i=PACK)
                nc.scalar.copy(rows[:, :, c * P:(c + 1) * P], bank[:, first:first + count, :])
            for n in range(count):
                y_rows[first + n, u] = rows[:, n, :]

        q_banks = {}

        def hazard_pass(b, c):
            if b == 0:
                tag, bufs = ("left", 2) if c < 2 else ("mid", 3)
                q_banks[c] = psum.tile([P, BANK], F32, name=tag, tag=tag, bufs=bufs)
            nc.tensor.matmul_mx(q_banks[c][:], lhsT=x_codes[b, c].bitcast(FP8X4), lhsT_scale=x_planes[b, c],
                                rhs=haz_sb[:, b, :].bitcast(FP8X4),
                                rhs_scale=haz_plane[:, b * N // 4:(b + 1) * N // 4].bitcast(U8),
                                start=(b == 0), stop=(b == blocks - 1))

        def score(c):
            dealt = q_banks[c][:].rearrange("m (p i) -> m i p", i=PACK)
            tanh_q = ring.tile([P, PACK, P], F32, name="tanh_q")
            nc.scalar.activation(tanh_q[:], dealt, ACT.Tanh)
            q_tide = ring.tile([P, PACK, P], F32, name="q_tide")
            nc.vector.tensor_tensor(q_tide[:], dealt, tide_t[c][:].rearrange("m (i p) -> m i p", i=PACK), ALU.mult)
            return tanh_q, q_tide

        def add_turned(c, terms):
            bank = psum.tile([P, BANK], F32, name="right", tag="right", bufs=3)
            for i in range(PACK):
                for n, term in enumerate(terms):
                    nc.tensor.matmul(bank[:, i * P:(i + 1) * P], lhsT=term[:, i, :], rhs=ident[:], is_transpose=True,
                                     start=(n == 0), stop=(n == 1))
            y_banks[c] = bank

        def place(i, u):
            nc.vector.tensor_tensor(pages[i][:].indirect(offs3_sb[:, u * OFFS_COLS:(u + 1) * OFFS_COLS]),
                                    y_rows[i, u], wgo_sb[:, u * HALF:(u + 1) * HALF], ALU.mult)

        for i in range(PACK):
            plume_sign(0, i)
            stronger(0, i)
        quantise_weight("view", 0, weave_weight("view", 0, "gpsimd"), pieces=2)
        woven_foam = weave_weight("foam", 1, "scalar")
        capped(0, 0)
        for i in range(1, PACK):
            capped(0, i)
            pick_early(0, i - 1)
            if i == 1:
                quantise_weight("foam", 1, woven_foam)
                plume_sign(1, 0)
                woven_view = weave_weight("view", 1, "scalar")
            plume_sign(1, i)
        stronger(1, 0)
        pick_early(0, PACK - 1)
        quantise_weight("view", 1, woven_view)
        woven = weave_x(0, 0, 2)
        for i in range(PACK):
            if i + 1 < PACK:
                stronger(1, i + 1)
            capped(1, i)
            if i == 0:
                quantise_x(0, 0, 2, woven)
            else:
                pick_early(1, i - 1)
            turn_tide(i)
        pick_early(1, PACK - 1)
        late = [(b, i) for b in range(blocks) for i in range(PACK)]
        first_late = keep.tile([P, 5, HALF], F32, name="first_late", tag="codes_view1", align_bytes=64)
        woven = [weave_x(1, c, 1) for c in range(2)]
        for c in range(2):
            hazard_pass(0, c)
        pick(*late[0], 1, first_late[:, 0, :])
        for c in range(2):
            pick(*late[1 + c], 1, first_late[:, 1 + c, :])
            quantise_x(1, c, 1, woven[c])
            hazard_pass(1, c)
        for n in range(3, 5):
            pick(*late[n], 1, first_late[:, n, :])
        for c in range(2):
            add_turned(c, score(c))
        make_y(0, 0, 2, "y_first")
        woven_first = weave_x(0, 2, 2)
        last_late = keep.tile([P, 3, HALF], F32, name="last_late", tag="tide_t0", align_bytes=64)
        for n in range(5, 8):
            pick(*late[n], 1, last_late[:, n - 5, :])
        woven = [weave_x(1, c, 1) for c in range(2, 4)]
        quantise_x(0, 2, 2, woven_first)
        for c in range(2, 4):
            hazard_pass(0, c)
        place(0, 0)
        place(1, 0)
        for c in range(2, 4):
            quantise_x(1, c, 1, woven[c - 2])
            hazard_pass(1, c)
        make_y(0, 2, 1, "x_rows11")
        place(2, 0)
        terms = [score(c) for c in range(2, 4)]
        make_y(0, 3, 1, "x_codes13")
        for c in range(2, 4):
            add_turned(c, terms[c - 2])
        place(3, 0)
        make_y(1, 0, PACK, "y_last")
        rows = out.rearrange("(p i) t -> p i t", i=PACK)
        for i in range(PACK):
            place(i, 1)
            nc.sync.dma_start(rows[:, i, :], pages[i][:])
